import numpy as np
import ml_dtypes


def mxq(x, axis, fmt="e4m3"):
    dtype, down = {"e4m3": (ml_dtypes.float8_e4m3fn, 7), "e5m2": (ml_dtypes.float8_e5m2, 14)}[fmt]
    v = np.moveaxis(np.asarray(x, np.float32).astype(ml_dtypes.bfloat16).astype(np.float64), axis, -1)
    blocks = v.reshape(v.shape[:-1] + (-1, 32))
    amax = np.abs(blocks).max(-1, keepdims=True)
    byte = np.maximum(np.where(amax > 0, np.frexp(amax)[1] - 1 + 127, 0) - down, 1)
    scale = np.exp2(byte - 127.0)
    codes = (blocks / scale).astype(np.float32).astype(dtype).astype(np.float64)
    return np.moveaxis((codes * scale).reshape(v.shape), -1, axis)


WIDE = False


def mx_kscale(k):
    if not WIDE:
        return np.ones(k)
    levels = np.array([10, -10, 5, -5, 0])
    if k % 512:
        return np.exp2(np.random.permutation(np.resize(levels, k // 32))).repeat(32)
    a = np.empty((k // 512, 16))
    for p in range(k // 512):
        a[p, :8] = np.random.permutation(np.resize(levels, 8))
        for g in range(8):
            far = levels[np.abs(levels - a[p, g]) >= 10]
            a[p, g + 8] = far[np.random.randint(len(far))]
    return np.exp2(a.ravel()).repeat(32)


def f64(x):
    return np.asarray(x).astype(np.float64)


def striped(idx):
    return np.tile(idx.reshape(-1, 16).T, (8, 1)).astype(np.uint16)


def unstriped(offs):
    return offs[:16].T.reshape(-1).astype(np.int64)


def pack_weight(w):
    k, n = w.shape
    w = f64(np.asarray(w, np.float32).astype(ml_dtypes.bfloat16)).reshape(k // 32, 32, n)
    amax = np.abs(w).max(1)
    byte = np.clip(np.where(amax > 0, np.frexp(amax)[1] - 1 + 127 - 7, 1), 1, 254)
    scaled = (w * np.exp2(127.0 - byte)[:, None, :]).reshape(k, n).astype(np.float32)
    words = np.ascontiguousarray(scaled.reshape(k // 512, 128, 4, n).transpose(0, 1, 3, 2)).astype(ml_dtypes.float8_e4m3fn).view(np.uint8)
    return words, np.ascontiguousarray(byte.astype(np.uint8).reshape(k // 512, 16, n))


def unpack_weight(words, scales):
    g, p, n, _ = words.shape
    vals = np.ascontiguousarray(words).view(ml_dtypes.float8_e4m3fn).astype(np.float64) * np.repeat(np.exp2(scales.astype(np.float64) - 127.0), 8, axis=1)[..., None]
    return vals.transpose(0, 1, 3, 2).reshape(g * 512, n)


K, T, S, V = 512, 1024, 512, 512


def setup_inputs():
    n = np.random.standard_normal
    s = mx_kscale(K)[:, None]
    packed_xT = pack_weight(n((K, T)) * s)
    return {
        "x_words": packed_xT[0],
        "x_scales": packed_xT[1],
        "hT": (n((K, V)) / np.sqrt(K) / s).astype(np.float32),
        "gT": (n((K, V)) / np.sqrt(K) / s).astype(np.float32),
        "ka": (0.5 * n((V, 3)) + 0.3).astype(np.float32),
        "offs": striped(np.random.permutation(T)[:S]),
    }


def reference(x_words, x_scales, hT, gT, ka, offs):
    hTq = mxq(f64(hT), 0, "e4m3")
    xq = unpack_weight(x_words, x_scales)[:, unstriped(offs)]
    y = hTq.T @ xq
    gTq = mxq(f64(gT), 0, "e4m3")
    z = gTq.T @ xq
    ww = f64(ka)[:, 0:1] * y + f64(ka)[:, 1:2] * (np.pad(y, ((0, 0), (1, 0)))[:, :S]) + f64(ka)[:, 2:3] * (np.pad(y, ((0, 0), (2, 0)))[:, :S]) + 0.5 * z
    ex = np.exp(ww - ww.max(axis=1, keepdims=True))
    return ex / ex.sum(axis=1, keepdims=True)

@@ -1,0 +1,99 @@
+from contextlib import ExitStack
+
+import concourse.mybir as mybir
+
+K, T, S, V = 512, 1024, 512, 512
+FLOPS = 2 * 2 * K * S * V
+
+F32 = mybir.dt.float32
+BF16 = mybir.dt.bfloat16
+I32 = mybir.dt.int32
+U32 = mybir.dt.uint32
+U16 = mybir.dt.uint16
+U8 = mybir.dt.uint8
+FP8X4 = mybir.dt.float8_e4m3fn_x4
+ALU = mybir.AluOpType
+ACT = mybir.ActivationFunctionType
+
+P = 128
+PACK = 4
+BLOCKS = V // P
+HALF = V // 2
+
+
+def tile_picked_ymta_one_p_kernel(tc, x_words, x_scales, hT, gT, ka, offs, out):
+    nc = tc.nc
+    with ExitStack() as ctx:
+        keep = ctx.enter_context(tc.tile_pool(name="keep", bufs=1))
+        psum = ctx.enter_context(tc.psum_pool(name="psum", bufs=1))
+
+        offsets = keep.tile([P, S // 16], U16, name="offsets")
+        nc.sync.dma_start(offsets[:], offs)
+
+        table_scales = keep.tile([P, T], U8, name="table_scales", align_bytes=64)
+        nc.vector.memset(table_scales[:].bitcast(I32), 0)
+        warm = keep.tile([P, 1], F32, name="warm")
+        nc.vector.memset(warm[:], 0.0)
+        warm_out = keep.tile([P, 1], F32, name="warm_out")
+        nc.scalar.activation(warm_out[:], warm[:], ACT.Exp)
+        for q in range(4):
+            nc.sync.dma_start(table_scales[32 * q : 32 * q + 4, :].bitcast(I32), x_scales[0, 4 * q : 4 * q + 4, :].bitcast(I32))
+        table_words = keep.tile([P, T], U32, name="table_words", align_bytes=64)
+        nc.sync.dma_start(table_words[:].bitcast(I32), x_words[0].rearrange("p n r -> p (n r)").bitcast(I32))
+
+        raw = {}
+        taps = keep.tile([P, BLOCKS, 3], F32, name="taps")
+        for half in range(2):
+            for name, src in (("h", hT), ("g", gT)):
+                raw[name, half] = keep.tile([P, PACK, HALF], F32, name=f"raw_{name}{half}", align_bytes=64)
+                nc.sync.dma_start(raw[name, half][:], src[:, half * HALF : (half + 1) * HALF].rearrange("(p j) w -> p j w", j=PACK))
+                if half == 0 and name == "h":
+                    nc.sync.dma_start(taps[:], ka.rearrange("(b p) c -> p b c", p=P))
+
+        key_scales = keep.tile([P, S], U8, name="key_scales", align_bytes=64)
+        nc.vector.tensor_copy(key_scales[:], table_scales[:].indirect(offsets[:]))
+        key_words = keep.tile([P, S], U32, name="key_words", align_bytes=64)
+        nc.vector.tensor_copy(key_words[:], table_words[:].indirect(offsets[:]))
+
+        scores = {}
+
+        def product(name, b):
+            half, part = divmod(b, 2)
+            grouped = keep.tile([P, P, PACK], BF16, name=f"grouped_{name}{b}", align_bytes=64)
+            nc.scalar.copy(
+                grouped[:].rearrange("p (c i) j -> p c j i", i=4),
+                raw[name, half][:, :, part * P : (part + 1) * P].rearrange("p j (c i) -> p c j i", i=4),
+            )
+            codes = keep.tile([P, P], U32, name=f"codes_{name}{b}", align_bytes=64)
+            scales = keep.tile([P, P], U8, name=f"scales_{name}{b}", align_bytes=64)
+            nc.vector.quantize_mx(out=codes[:].bitcast(FP8X4), scales=scales[:], in_=grouped[:].rearrange("p w j -> p (w j)"))
+            scores[name, b] = psum.tile([P, S], F32, name=f"scores_{name}{b}")
+            nc.tensor.matmul_mx(
+                out=scores[name, b][:], lhsT=codes[:].bitcast(FP8X4), lhsT_scale=scales[:],
+                rhs=key_words[:].bitcast(FP8X4), rhs_scale=key_scales[:], start=True, stop=True,
+            )
+
+        def softmax(b):
+            y, z = scores["h", b], scores["g", b]
+            ww = keep.tile([P, S], F32, name=f"ww{b}")
+            nc.scalar.activation(ww[:], y[:], ACT.Copy, scale=taps[:, b, 0:1])
+            for lag in (1, 2):
+                nc.vector.scalar_tensor_tensor(ww[:, lag:], y[:, : S - lag], taps[:, b, lag : lag + 1], ww[:, lag:], ALU.mult, ALU.add)
+            nc.vector.scalar_tensor_tensor(ww[:], z[:], 0.5, ww[:], ALU.mult, ALU.add)
+            neg_max = keep.tile([P, 1], F32, name=f"neg_max{b}")
+            nc.vector.tensor_reduce(neg_max[:], ww[:], mybir.AxisListType.X, ALU.max, negate=True)
+            ex = keep.tile([P, S], F32, name=f"ex{b}")
+            total = keep.tile([P, 1], F32, name=f"total{b}")
+            nc.scalar.activation(ex[:], ww[:], ACT.Exp, bias=neg_max[:], scale=1.0, accum_out=total[:])
+            inv = keep.tile([P, 1], F32, name=f"inv{b}")
+            nc.vector.reciprocal(inv[:], total[:])
+            res = keep.tile([P, S], F32, name=f"res{b}")
+            nc.gpsimd.tensor_scalar(res[:], ex[:], inv[:], 0.0, ALU.mult, ALU.add)
+            nc.sync.dma_start(out[b * P : (b + 1) * P, :], res[:])
+
+        for half in range(2):
+            for name in ("h", "g"):
+                for part in range(2):
+                    product(name, 2 * half + part)
+            for part in range(2):
+                softmax(2 * half + part)

@@ -36,64 +36,104 @@ def tile_picked_ymta_one_p_kernel(tc, x_words, x_scales, hT, gT, ka, offs, out):
         nc.vector.memset(warm[:], 0.0)
         warm_out = keep.tile([P, 1], F32, name="warm_out")
         nc.scalar.activation(warm_out[:], warm[:], ACT.Exp)
-        for q in range(4):
-            nc.sync.dma_start(table_scales[32 * q : 32 * q + 4, :].bitcast(I32), x_scales[0, 4 * q : 4 * q + 4, :].bitcast(I32))
         table_words = keep.tile([P, T], U32, name="table_words", align_bytes=64)
         nc.sync.dma_start(table_words[:].bitcast(I32), x_words[0].rearrange("p n r -> p (n r)").bitcast(I32))
+        for q in range(4):
+            nc.sync.dma_start(table_scales[32 * q : 32 * q + 4, :].bitcast(I32), x_scales[0, 4 * q : 4 * q + 4, :].bitcast(I32))
 
         raw = {}
         taps = keep.tile([P, BLOCKS, 3], F32, name="taps")
         for half in range(2):
             for name, src in (("h", hT), ("g", gT)):
-                raw[name, half] = keep.tile([P, PACK, HALF], F32, name=f"raw_{name}{half}", align_bytes=64)
+                raw[name, half] = keep.tile([P, PACK, HALF], F32, name=f"raw_{name}{half}", tag=f"raw_{name}{half}", align_bytes=64)
                 nc.sync.dma_start(raw[name, half][:], src[:, half * HALF : (half + 1) * HALF].rearrange("(p j) w -> p j w", j=PACK))
-                if half == 0 and name == "h":
+                if half == 0 and name == "g":
                     nc.sync.dma_start(taps[:], ka.rearrange("(b p) c -> p b c", p=P))
 
-        key_scales = keep.tile([P, S], U8, name="key_scales", align_bytes=64)
-        nc.vector.tensor_copy(key_scales[:], table_scales[:].indirect(offsets[:]))
         key_words = keep.tile([P, S], U32, name="key_words", align_bytes=64)
         nc.vector.tensor_copy(key_words[:], table_words[:].indirect(offsets[:]))
+        key_scales = keep.tile([P, S], U8, name="key_scales", align_bytes=64)
+        nc.vector.tensor_copy(key_scales[:], table_scales[:].indirect(offsets[:]))
 
-        scores = {}
+        scores, part, halfz, ww, neg_max = {}, {}, {}, {}, {}
 
-        def product(name, b):
-            half, part = divmod(b, 2)
-            grouped = keep.tile([P, P, PACK], BF16, name=f"grouped_{name}{b}", align_bytes=64)
-            nc.scalar.copy(
-                grouped[:].rearrange("p (c i) j -> p c j i", i=4),
-                raw[name, half][:, :, part * P : (part + 1) * P].rearrange("p j (c i) -> p c j i", i=4),
-            )
-            codes = keep.tile([P, P], U32, name=f"codes_{name}{b}", align_bytes=64)
-            scales = keep.tile([P, P], U8, name=f"scales_{name}{b}", align_bytes=64)
+        def products(name, half, on_vector):
+            src = raw[name, half]
+            grouped = keep.tile([P, HALF, PACK], BF16, name=f"grouped_{name}{half}", tag=f"stage_{name}{half}", align_bytes=64)
+            if on_vector:
+                nc.vector.tensor_copy(grouped[:].rearrange("p (c i) j -> p c j i", i=4), src[:].rearrange("p j (c i) -> p c j i", i=4))
+            else:
+                nc.scalar.copy(grouped[:, :P, :].rearrange("p (c i) j -> p c j i", i=4), src[:, :, :P].rearrange("p j (c i) -> p c j i", i=4))
+                nc.gpsimd.tensor_scalar(grouped[:, P:, :], src[:, :, P:].rearrange("p j w -> p w j"), 1.0, 0.0, ALU.mult, ALU.add)
+            codes = keep.tile([P, HALF], U32, name=f"codes_{name}{half}", align_bytes=64)
+            scales = keep.tile([P, HALF], U8, name=f"scales_{name}{half}", align_bytes=64)
             nc.vector.quantize_mx(out=codes[:].bitcast(FP8X4), scales=scales[:], in_=grouped[:].rearrange("p w j -> p (w j)"))
-            scores[name, b] = psum.tile([P, S], F32, name=f"scores_{name}{b}")
-            nc.tensor.matmul_mx(
-                out=scores[name, b][:], lhsT=codes[:].bitcast(FP8X4), lhsT_scale=scales[:],
-                rhs=key_words[:].bitcast(FP8X4), rhs_scale=key_scales[:], start=True, stop=True,
-            )
+            for b in (2 * half, 2 * half + 1):
+                cols = slice(b % 2 * P, (b % 2 + 1) * P)
+                scores[name, b] = psum.tile([P, S], F32, name=f"scores_{name}{b}")
+                nc.tensor.matmul_mx(
+                    out=scores[name, b][:], lhsT=codes[:, cols].bitcast(FP8X4), lhsT_scale=scales[:, cols],
+                    rhs=key_words[:].bitcast(FP8X4), rhs_scale=key_scales[:], start=True, stop=True,
+                )
+
+        def tap0(b):
+            part[b] = keep.tile([P, S], F32, name=f"part{b}")
+            nc.scalar.activation(part[b][:], scores["h", b][:], ACT.Copy, scale=taps[:, b, 0:1])
+
+        def tap(b, lag):
+            nc.vector.scalar_tensor_tensor(part[b][:, lag:], scores["h", b][:, : S - lag], taps[:, b, lag : lag + 1], part[b][:, lag:], ALU.mult, ALU.add)
+
+        def add_z_gpsimd(b):
+            halfz[b] = keep.tile([P, S], F32, name=f"halfz{b}")
+            nc.scalar.activation(halfz[b][:], scores["g", b][:], ACT.Copy, scale=0.5)
+            if b == 0:
+                ww[b] = keep.tile([P, S], F32, name=f"ww{b}", tag="stage_g1", align_bytes=64)
+            else:
+                ww[b] = keep.tile([P, S], F32, name=f"ww{b}")
+            nc.gpsimd.tensor_tensor(ww[b][:], part[b][:], halfz[b][:], ALU.add)
+
+        def add_z_vector(b):
+            ww[b] = part[b]
+            nc.vector.scalar_tensor_tensor(ww[b][:], scores["g", b][:], 0.5, ww[b][:], ALU.mult, ALU.add)
 
         def softmax(b):
-            y, z = scores["h", b], scores["g", b]
-            ww = keep.tile([P, S], F32, name=f"ww{b}")
-            nc.scalar.activation(ww[:], y[:], ACT.Copy, scale=taps[:, b, 0:1])
-            for lag in (1, 2):
-                nc.vector.scalar_tensor_tensor(ww[:, lag:], y[:, : S - lag], taps[:, b, lag : lag + 1], ww[:, lag:], ALU.mult, ALU.add)
-            nc.vector.scalar_tensor_tensor(ww[:], z[:], 0.5, ww[:], ALU.mult, ALU.add)
             neg_max = keep.tile([P, 1], F32, name=f"neg_max{b}")
-            nc.vector.tensor_reduce(neg_max[:], ww[:], mybir.AxisListType.X, ALU.max, negate=True)
+            nc.vector.tensor_reduce(neg_max[:], ww[b][:], mybir.AxisListType.X, ALU.max, negate=True)
             ex = keep.tile([P, S], F32, name=f"ex{b}")
             total = keep.tile([P, 1], F32, name=f"total{b}")
-            nc.scalar.activation(ex[:], ww[:], ACT.Exp, bias=neg_max[:], scale=1.0, accum_out=total[:])
+            nc.scalar.activation(ex[:], ww[b][:], ACT.Exp, bias=neg_max[:], scale=1.0, accum_out=total[:])
             inv = keep.tile([P, 1], F32, name=f"inv{b}")
             nc.vector.reciprocal(inv[:], total[:])
             res = keep.tile([P, S], F32, name=f"res{b}")
-            nc.gpsimd.tensor_scalar(res[:], ex[:], inv[:], 0.0, ALU.mult, ALU.add)
+            if b == BLOCKS - 1:
+                nc.vector.tensor_scalar(res[:], ex[:], inv[:], None, ALU.mult)
+            elif b == 0:
+                nc.scalar.activation(res[:], ex[:], ACT.Copy, scale=inv[:])
+            else:
+                nc.gpsimd.tensor_scalar(res[:], ex[:], inv[:], 0.0, ALU.mult, ALU.add)
             nc.sync.dma_start(out[b * P : (b + 1) * P, :], res[:])
 
-        for half in range(2):
-            for name in ("h", "g"):
-                for part in range(2):
-                    product(name, 2 * half + part)
-            for part in range(2):
-                softmax(2 * half + part)
+        products("h", 0, False)
+        products("g", 0, False)
+        tap0(0)
+        tap0(1)
+        products("h", 1, True)
+        products("g", 1, False)
+        tap(0, 1)
+        tap(0, 2)
+        add_z_gpsimd(0)
+        tap0(2)
+        tap(1, 1)
+        tap(2, 1)
+        tap(1, 2)
+        add_z_gpsimd(1)
+        tap0(3)
+        softmax(0)
+        tap(2, 2)
+        add_z_gpsimd(2)
+        tap(3, 1)
+        softmax(1)
+        tap(3, 2)
+        softmax(2)
+        add_z_vector(3)
+        softmax(3)

@@ -17,8 +17,12 @@ ACT = mybir.ActivationFunctionType
 
 P = 128
 PACK = 4
+QUADRANTS = 4
+TAPS = 3
 BLOCKS = V // P
+LAST = BLOCKS - 1
 HALF = V // 2
+RUN = 4
 
 
 def tile_picked_ymta_one_p_kernel(tc, x_words, x_scales, hT, gT, ka, offs, out):
@@ -32,38 +36,34 @@ def tile_picked_ymta_one_p_kernel(tc, x_words, x_scales, hT, gT, ka, offs, out):
 
         table_scales = keep.tile([P, T], U8, name="table_scales", align_bytes=64)
         nc.vector.memset(table_scales[:].bitcast(I32), 0)
-        warm = keep.tile([P, 1], F32, name="warm")
-        nc.vector.memset(warm[:], 0.0)
-        warm_out = keep.tile([P, 1], F32, name="warm_out")
-        nc.scalar.activation(warm_out[:], warm[:], ACT.Exp)
         table_words = keep.tile([P, T], U32, name="table_words", align_bytes=64)
         nc.sync.dma_start(table_words[:].bitcast(I32), x_words[0].rearrange("p n r -> p (n r)").bitcast(I32))
-        for q in range(4):
+        for q in range(QUADRANTS):
             nc.sync.dma_start(table_scales[32 * q : 32 * q + 4, :].bitcast(I32), x_scales[0, 4 * q : 4 * q + 4, :].bitcast(I32))
 
         raw = {}
-        taps = keep.tile([P, BLOCKS, 3], F32, name="taps")
+        taps = keep.tile([P, BLOCKS, TAPS], F32, name="taps")
         for half in range(2):
             for name, src in (("h", hT), ("g", gT)):
-                raw[name, half] = keep.tile([P, PACK, HALF], F32, name=f"raw_{name}{half}", tag=f"raw_{name}{half}", align_bytes=64)
+                raw[name, half] = keep.tile([P, PACK, HALF], F32, name=f"raw_{name}{half}", align_bytes=64)
                 nc.sync.dma_start(raw[name, half][:], src[:, half * HALF : (half + 1) * HALF].rearrange("(p j) w -> p j w", j=PACK))
-                if half == 0 and name == "g":
-                    nc.sync.dma_start(taps[:], ka.rearrange("(b p) c -> p b c", p=P))
+            if half == 0:
+                nc.sync.dma_start(taps[:], ka.rearrange("(b p) c -> p b c", p=P))
 
         key_words = keep.tile([P, S], U32, name="key_words", align_bytes=64)
         nc.vector.tensor_copy(key_words[:], table_words[:].indirect(offsets[:]))
         key_scales = keep.tile([P, S], U8, name="key_scales", align_bytes=64)
         nc.vector.tensor_copy(key_scales[:], table_scales[:].indirect(offsets[:]))
 
-        scores, part, halfz, ww, neg_max = {}, {}, {}, {}, {}
+        scores, filtered, logits, exps, sums = {}, {}, {}, {}, {}
 
-        def products(name, half, on_vector):
+        def products(name, half, round_on_vector):
             src = raw[name, half]
             grouped = keep.tile([P, HALF, PACK], BF16, name=f"grouped_{name}{half}", tag=f"stage_{name}{half}", align_bytes=64)
-            if on_vector:
-                nc.vector.tensor_copy(grouped[:].rearrange("p (c i) j -> p c j i", i=4), src[:].rearrange("p j (c i) -> p c j i", i=4))
+            if round_on_vector:
+                nc.vector.tensor_copy(grouped[:].rearrange("p (c i) j -> p c j i", i=RUN), src[:].rearrange("p j (c i) -> p c j i", i=RUN))
             else:
-                nc.scalar.copy(grouped[:, :P, :].rearrange("p (c i) j -> p c j i", i=4), src[:, :, :P].rearrange("p j (c i) -> p c j i", i=4))
+                nc.scalar.activation(grouped[:, :P, :].rearrange("p (c i) j -> p c j i", i=RUN), src[:, :, :P].rearrange("p j (c i) -> p c j i", i=RUN), ACT.Copy)
                 nc.gpsimd.tensor_scalar(grouped[:, P:, :], src[:, :, P:].rearrange("p j w -> p w j"), 1.0, 0.0, ALU.mult, ALU.add)
             codes = keep.tile([P, HALF], U32, name=f"codes_{name}{half}", align_bytes=64)
             scales = keep.tile([P, HALF], U8, name=f"scales_{name}{half}", align_bytes=64)
@@ -72,68 +72,76 @@ def tile_picked_ymta_one_p_kernel(tc, x_words, x_scales, hT, gT, ka, offs, out):
                 cols = slice(b % 2 * P, (b % 2 + 1) * P)
                 scores[name, b] = psum.tile([P, S], F32, name=f"scores_{name}{b}")
                 nc.tensor.matmul_mx(
-                    out=scores[name, b][:], lhsT=codes[:, cols].bitcast(FP8X4), lhsT_scale=scales[:, cols],
-                    rhs=key_words[:].bitcast(FP8X4), rhs_scale=key_scales[:], start=True, stop=True,
+                    out=scores[name, b][:],
+                    lhsT=codes[:, cols].bitcast(FP8X4),
+                    lhsT_scale=scales[:, cols],
+                    rhs=key_words[:].bitcast(FP8X4),
+                    rhs_scale=key_scales[:],
+                    start=True,
+                    stop=True,
                 )
 
-        def tap0(b):
-            part[b] = keep.tile([P, S], F32, name=f"part{b}")
-            nc.scalar.activation(part[b][:], scores["h", b][:], ACT.Copy, scale=taps[:, b, 0:1])
+        def first_tap(b):
+            filtered[b] = keep.tile([P, S], F32, name=f"filtered{b}")
+            nc.scalar.activation(filtered[b][:], scores["h", b][:], ACT.Copy, scale=taps[:, b, 0:1])
 
-        def tap(b, lag):
-            nc.vector.scalar_tensor_tensor(part[b][:, lag:], scores["h", b][:, : S - lag], taps[:, b, lag : lag + 1], part[b][:, lag:], ALU.mult, ALU.add)
+        def lagged_tap(b, lag):
+            nc.vector.scalar_tensor_tensor(
+                filtered[b][:, lag:], scores["h", b][:, : S - lag], taps[:, b, lag : lag + 1], filtered[b][:, lag:], ALU.mult, ALU.add
+            )
 
-        def add_z_gpsimd(b):
-            halfz[b] = keep.tile([P, S], F32, name=f"halfz{b}")
-            nc.scalar.activation(halfz[b][:], scores["g", b][:], ACT.Copy, scale=0.5)
-            if b == 0:
-                ww[b] = keep.tile([P, S], F32, name=f"ww{b}", tag="stage_g1", align_bytes=64)
-            else:
-                ww[b] = keep.tile([P, S], F32, name=f"ww{b}")
-            nc.gpsimd.tensor_tensor(ww[b][:], part[b][:], halfz[b][:], ALU.add)
+        def add_z_on_gpsimd(b):
+            half_z = keep.tile([P, S], F32, name=f"half_z{b}")
+            nc.scalar.activation(half_z[:], scores["g", b][:], ACT.Copy, scale=0.5)
+            logits[b] = keep.tile([P, S], F32, name=f"logits{b}", tag="stage_g1" if b == 0 else f"logits{b}", align_bytes=64)
+            nc.gpsimd.tensor_tensor(logits[b][:], filtered[b][:], half_z[:], ALU.add)
 
-        def add_z_vector(b):
-            ww[b] = part[b]
-            nc.vector.scalar_tensor_tensor(ww[b][:], scores["g", b][:], 0.5, ww[b][:], ALU.mult, ALU.add)
+        def add_z_on_vector(b):
+            logits[b] = filtered[b]
+            nc.vector.scalar_tensor_tensor(logits[b][:], scores["g", b][:], 0.5, logits[b][:], ALU.mult, ALU.add)
 
-        def softmax(b):
+        def exponentials(b):
             neg_max = keep.tile([P, 1], F32, name=f"neg_max{b}")
-            nc.vector.tensor_reduce(neg_max[:], ww[b][:], mybir.AxisListType.X, ALU.max, negate=True)
-            ex = keep.tile([P, S], F32, name=f"ex{b}")
-            total = keep.tile([P, 1], F32, name=f"total{b}")
-            nc.scalar.activation(ex[:], ww[b][:], ACT.Exp, bias=neg_max[:], scale=1.0, accum_out=total[:])
-            inv = keep.tile([P, 1], F32, name=f"inv{b}")
-            nc.vector.reciprocal(inv[:], total[:])
-            res = keep.tile([P, S], F32, name=f"res{b}")
-            if b == BLOCKS - 1:
-                nc.vector.tensor_scalar(res[:], ex[:], inv[:], None, ALU.mult)
-            elif b == 0:
-                nc.scalar.activation(res[:], ex[:], ACT.Copy, scale=inv[:])
-            else:
-                nc.gpsimd.tensor_scalar(res[:], ex[:], inv[:], 0.0, ALU.mult, ALU.add)
-            nc.sync.dma_start(out[b * P : (b + 1) * P, :], res[:])
+            nc.vector.tensor_reduce(neg_max[:], logits[b][:], mybir.AxisListType.X, ALU.max, negate=True)
+            exps[b] = keep.tile([P, S], F32, name=f"exps{b}")
+            sums[b] = keep.tile([P, 1], F32, name=f"sums{b}")
+            nc.scalar.activation(exps[b][:], logits[b][:], ACT.Exp, bias=neg_max[:], scale=1.0, accum_out=sums[b][:])
 
-        products("h", 0, False)
-        products("g", 0, False)
-        tap0(0)
-        tap0(1)
-        products("h", 1, True)
-        products("g", 1, False)
-        tap(0, 1)
-        tap(0, 2)
-        add_z_gpsimd(0)
-        tap0(2)
-        tap(1, 1)
-        tap(2, 1)
-        tap(1, 2)
-        add_z_gpsimd(1)
-        tap0(3)
-        softmax(0)
-        tap(2, 2)
-        add_z_gpsimd(2)
-        tap(3, 1)
-        softmax(1)
-        tap(3, 2)
-        softmax(2)
-        add_z_vector(3)
-        softmax(3)
+        def normalise(b, on_gpsimd, pieces):
+            inverse = keep.tile([P, 1], F32, name=f"inverse{b}")
+            nc.vector.reciprocal(inverse[:], sums[b][:])
+            width = S // pieces
+            for n in range(pieces):
+                cols = slice(n * width, (n + 1) * width)
+                result = keep.tile([P, width], F32, name=f"result{b}_{n}")
+                if on_gpsimd:
+                    nc.gpsimd.tensor_scalar(result[:], exps[b][:, cols], inverse[:], 0.0, ALU.mult, ALU.add)
+                else:
+                    nc.vector.tensor_scalar(result[:], exps[b][:, cols], inverse[:], None, ALU.mult)
+                nc.sync.dma_start(out[b * P : (b + 1) * P, cols], result[:])
+
+        products("h", 0, round_on_vector=False)
+        products("g", 0, round_on_vector=False)
+        first_tap(0)
+        first_tap(1)
+        products("h", 1, round_on_vector=True)
+        products("g", 1, round_on_vector=False)
+
+        lagged_tap(0, 1)
+        for b in range(LAST):
+            lagged_tap(b + 1, 1)
+            lagged_tap(b, 2)
+            add_z_on_gpsimd(b)
+            if b == 0:
+                first_tap(2)
+                first_tap(3)
+
+        exponentials(0)
+        lagged_tap(LAST, 2)
+        normalise(0, on_gpsimd=True, pieces=1)
+        exponentials(1)
+        add_z_on_vector(LAST)
+        exponentials(2)
+        exponentials(LAST)
+        for b in range(1, BLOCKS):
+            normalise(b, on_gpsimd=False, pieces=2 if b == LAST else 1)

@@ -19,6 +19,7 @@ P = 128
 PACK = 4
 QUADRANTS = 4
 TAPS = 3
+TAP_ROW = 8
 BLOCKS = V // P
 LAST = BLOCKS - 1
 HALF = V // 2
@@ -42,13 +43,13 @@ def tile_picked_ymta_one_p_kernel(tc, x_words, x_scales, hT, gT, ka, offs, out):
             nc.sync.dma_start(table_scales[32 * q : 32 * q + 4, :].bitcast(I32), x_scales[0, 4 * q : 4 * q + 4, :].bitcast(I32))
 
         raw = {}
-        taps = keep.tile([P, BLOCKS, TAPS], F32, name="taps")
+        taps = keep.tile([P, BLOCKS, TAP_ROW], F32, name="taps")
         for half in range(2):
             for name, src in (("h", hT), ("g", gT)):
                 raw[name, half] = keep.tile([P, PACK, HALF], F32, name=f"raw_{name}{half}", align_bytes=64)
                 nc.sync.dma_start(raw[name, half][:], src[:, half * HALF : (half + 1) * HALF].rearrange("(p j) w -> p j w", j=PACK))
             if half == 0:
-                nc.sync.dma_start(taps[:], ka.rearrange("(b p) c -> p b c", p=P))
+                nc.sync.dma_start(taps[:, :, :TAPS], ka.rearrange("(b p) c -> p b c", p=P))
 
         key_words = keep.tile([P, S], U32, name="key_words", align_bytes=64)
         nc.vector.tensor_copy(key_words[:], table_words[:].indirect(offsets[:]))
@@ -57,19 +58,30 @@ def tile_picked_ymta_one_p_kernel(tc, x_words, x_scales, hT, gT, ka, offs, out):
 
         scores, filtered, logits, exps, sums = {}, {}, {}, {}, {}
 
-        def products(name, half, round_on_vector):
-            src = raw[name, half]
-            grouped = keep.tile([P, HALF, PACK], BF16, name=f"grouped_{name}{half}", tag=f"stage_{name}{half}", align_bytes=64)
-            if round_on_vector:
-                nc.vector.tensor_copy(grouped[:].rearrange("p (c i) j -> p c j i", i=RUN), src[:].rearrange("p j (c i) -> p c j i", i=RUN))
+        def round_block(engine, target, source):
+            if engine == "gpsimd":
+                nc.gpsimd.tensor_scalar(target, source.rearrange("p j w -> p w j"), 1.0, 0.0, ALU.mult, ALU.add)
+                return
+            target = target.rearrange("p (c i) j -> p c j i", i=RUN)
+            source = source.rearrange("p j (c i) -> p c j i", i=RUN)
+            if engine == "scalar":
+                nc.scalar.activation(target, source, ACT.Copy)
             else:
-                nc.scalar.activation(grouped[:, :P, :].rearrange("p (c i) j -> p c j i", i=RUN), src[:, :, :P].rearrange("p j (c i) -> p c j i", i=RUN), ACT.Copy)
-                nc.gpsimd.tensor_scalar(grouped[:, P:, :], src[:, :, P:].rearrange("p j w -> p w j"), 1.0, 0.0, ALU.mult, ALU.add)
-            codes = keep.tile([P, HALF], U32, name=f"codes_{name}{half}", align_bytes=64)
-            scales = keep.tile([P, HALF], U8, name=f"scales_{name}{half}", align_bytes=64)
+                nc.vector.tensor_copy(target, source)
+
+        def products(name, blocks, engines, stage):
+            width = len(blocks) * P
+            source = raw[name, blocks[0] // 2][:, :, blocks[0] % 2 * P : blocks[0] % 2 * P + width]
+            grouped = keep.tile([P, width, PACK], BF16, name=f"grouped_{name}{blocks[0]}", tag=stage, align_bytes=64)
+            share = width // len(engines)
+            for n, engine in enumerate(engines):
+                cols = slice(n * share, (n + 1) * share)
+                round_block(engine, grouped[:, cols, :], source[:, :, cols])
+            codes = keep.tile([P, width], U32, name=f"codes_{name}{blocks[0]}", align_bytes=64)
+            scales = keep.tile([P, width], U8, name=f"scales_{name}{blocks[0]}", align_bytes=64)
             nc.vector.quantize_mx(out=codes[:].bitcast(FP8X4), scales=scales[:], in_=grouped[:].rearrange("p w j -> p (w j)"))
-            for b in (2 * half, 2 * half + 1):
-                cols = slice(b % 2 * P, (b % 2 + 1) * P)
+            for n, b in enumerate(blocks):
+                cols = slice(n * P, (n + 1) * P)
                 scores[name, b] = psum.tile([P, S], F32, name=f"scores_{name}{b}")
                 nc.tensor.matmul_mx(
                     out=scores[name, b][:],
@@ -93,7 +105,7 @@ def tile_picked_ymta_one_p_kernel(tc, x_words, x_scales, hT, gT, ka, offs, out):
         def add_z_on_gpsimd(b):
             half_z = keep.tile([P, S], F32, name=f"half_z{b}")
             nc.scalar.activation(half_z[:], scores["g", b][:], ACT.Copy, scale=0.5)
-            logits[b] = keep.tile([P, S], F32, name=f"logits{b}", tag="stage_g1" if b == 0 else f"logits{b}", align_bytes=64)
+            logits[b] = keep.tile([P, S], F32, name=f"logits{b}", tag="stage_last" if b == 0 else f"logits{b}", align_bytes=64)
             nc.gpsimd.tensor_tensor(logits[b][:], filtered[b][:], half_z[:], ALU.add)
 
         def add_z_on_vector(b):
@@ -120,12 +132,13 @@ def tile_picked_ymta_one_p_kernel(tc, x_words, x_scales, hT, gT, ka, offs, out):
                     nc.vector.tensor_scalar(result[:], exps[b][:, cols], inverse[:], None, ALU.mult)
                 nc.sync.dma_start(out[b * P : (b + 1) * P, cols], result[:])
 
-        products("h", 0, round_on_vector=False)
-        products("g", 0, round_on_vector=False)
+        products("h", [0, 1], ["scalar", "gpsimd"], "stage_first")
+        products("g", [0], ["scalar"], "stage_g0")
+        products("g", [1], ["vector"], "stage_first")
         first_tap(0)
         first_tap(1)
-        products("h", 1, round_on_vector=True)
-        products("g", 1, round_on_vector=False)
+        products("h", [2, 3], ["vector"], "stage_h2")
+        products("g", [2, 3], ["scalar", "gpsimd"], "stage_last")
 
         lagged_tap(0, 1)
         for b in range(LAST):

from contextlib import ExitStack

import concourse.mybir as mybir

K, T, S, V = 512, 1024, 512, 512
FLOPS = 2 * 2 * K * S * V

F32 = mybir.dt.float32
BF16 = mybir.dt.bfloat16
I32 = mybir.dt.int32
U32 = mybir.dt.uint32
U16 = mybir.dt.uint16
U8 = mybir.dt.uint8
FP8X4 = mybir.dt.float8_e4m3fn_x4
ALU = mybir.AluOpType
ACT = mybir.ActivationFunctionType

P = 128
PACK = 4
QUADRANTS = 4
TAPS = 3
TAP_ROW = 8
BLOCKS = V // P
LAST = BLOCKS - 1
HALF = V // 2
RUN = 4


def tile_picked_ymta_one_p_kernel(tc, x_words, x_scales, hT, gT, ka, offs, out):
    nc = tc.nc
    with ExitStack() as ctx:
        keep = ctx.enter_context(tc.tile_pool(name="keep", bufs=1))
        psum = ctx.enter_context(tc.psum_pool(name="psum", bufs=1))

        offsets = keep.tile([P, S // 16], U16, name="offsets")
        nc.sync.dma_start(offsets[:], offs)

        table_scales = keep.tile([P, T], U8, name="table_scales", align_bytes=64)
        nc.vector.memset(table_scales[:].bitcast(I32), 0)
        table_words = keep.tile([P, T], U32, name="table_words", align_bytes=64)
        nc.sync.dma_start(table_words[:].bitcast(I32), x_words[0].rearrange("p n r -> p (n r)").bitcast(I32))
        for q in range(QUADRANTS):
            nc.sync.dma_start(table_scales[32 * q : 32 * q + 4, :].bitcast(I32), x_scales[0, 4 * q : 4 * q + 4, :].bitcast(I32))

        raw = {}
        taps = keep.tile([P, BLOCKS, TAP_ROW], F32, name="taps")
        for half in range(2):
            for name, src in (("h", hT), ("g", gT)):
                raw[name, half] = keep.tile([P, PACK, HALF], F32, name=f"raw_{name}{half}", align_bytes=64)
                nc.sync.dma_start(raw[name, half][:], src[:, half * HALF : (half + 1) * HALF].rearrange("(p j) w -> p j w", j=PACK))
            if half == 0:
                nc.sync.dma_start(taps[:, :, :TAPS], ka.rearrange("(b p) c -> p b c", p=P))

        key_words = keep.tile([P, S], U32, name="key_words", align_bytes=64)
        nc.vector.tensor_copy(key_words[:], table_words[:].indirect(offsets[:]))
        key_scales = keep.tile([P, S], U8, name="key_scales", align_bytes=64)
        nc.vector.tensor_copy(key_scales[:], table_scales[:].indirect(offsets[:]))

        scores, filtered, logits, exps, sums = {}, {}, {}, {}, {}

        def round_block(engine, target, source):
            if engine == "gpsimd":
                nc.gpsimd.tensor_scalar(target, source.rearrange("p j w -> p w j"), 1.0, 0.0, ALU.mult, ALU.add)
                return
            target = target.rearrange("p (c i) j -> p c j i", i=RUN)
            source = source.rearrange("p j (c i) -> p c j i", i=RUN)
            if engine == "scalar":
                nc.scalar.activation(target, source, ACT.Copy)
            else:
                nc.vector.tensor_copy(target, source)

        def products(name, blocks, engines, stage):
            width = len(blocks) * P
            source = raw[name, blocks[0] // 2][:, :, blocks[0] % 2 * P : blocks[0] % 2 * P + width]
            grouped = keep.tile([P, width, PACK], BF16, name=f"grouped_{name}{blocks[0]}", tag=stage, align_bytes=64)
            share = width // len(engines)
            for n, engine in enumerate(engines):
                cols = slice(n * share, (n + 1) * share)
                round_block(engine, grouped[:, cols, :], source[:, :, cols])
            codes = keep.tile([P, width], U32, name=f"codes_{name}{blocks[0]}", align_bytes=64)
            scales = keep.tile([P, width], U8, name=f"scales_{name}{blocks[0]}", align_bytes=64)
            nc.vector.quantize_mx(out=codes[:].bitcast(FP8X4), scales=scales[:], in_=grouped[:].rearrange("p w j -> p (w j)"))
            for n, b in enumerate(blocks):
                cols = slice(n * P, (n + 1) * P)
                scores[name, b] = psum.tile([P, S], F32, name=f"scores_{name}{b}")
                nc.tensor.matmul_mx(
                    out=scores[name, b][:],
                    lhsT=codes[:, cols].bitcast(FP8X4),
                    lhsT_scale=scales[:, cols],
                    rhs=key_words[:].bitcast(FP8X4),
                    rhs_scale=key_scales[:],
                    start=True,
                    stop=True,
                )

        def first_tap(b):
            filtered[b] = keep.tile([P, S], F32, name=f"filtered{b}")
            nc.scalar.activation(filtered[b][:], scores["h", b][:], ACT.Copy, scale=taps[:, b, 0:1])

        def lagged_tap(b, lag):
            nc.vector.scalar_tensor_tensor(
                filtered[b][:, lag:], scores["h", b][:, : S - lag], taps[:, b, lag : lag + 1], filtered[b][:, lag:], ALU.mult, ALU.add
            )

        def add_z_on_gpsimd(b):
            half_z = keep.tile([P, S], F32, name=f"half_z{b}")
            nc.scalar.activation(half_z[:], scores["g", b][:], ACT.Copy, scale=0.5)
            logits[b] = keep.tile([P, S], F32, name=f"logits{b}", tag="stage_last" if b == 0 else f"logits{b}", align_bytes=64)
            nc.gpsimd.tensor_tensor(logits[b][:], filtered[b][:], half_z[:], ALU.add)

        def add_z_on_vector(b):
            logits[b] = filtered[b]
            nc.vector.scalar_tensor_tensor(logits[b][:], scores["g", b][:], 0.5, logits[b][:], ALU.mult, ALU.add)

        def exponentials(b):
            neg_max = keep.tile([P, 1], F32, name=f"neg_max{b}")
            nc.vector.tensor_reduce(neg_max[:], logits[b][:], mybir.AxisListType.X, ALU.max, negate=True)
            exps[b] = keep.tile([P, S], F32, name=f"exps{b}")
            sums[b] = keep.tile([P, 1], F32, name=f"sums{b}")
            nc.scalar.activation(exps[b][:], logits[b][:], ACT.Exp, bias=neg_max[:], scale=1.0, accum_out=sums[b][:])

        def normalise(b, on_gpsimd, pieces):
            inverse = keep.tile([P, 1], F32, name=f"inverse{b}")
            nc.vector.reciprocal(inverse[:], sums[b][:])
            width = S // pieces
            for n in range(pieces):
                cols = slice(n * width, (n + 1) * width)
                result = keep.tile([P, width], F32, name=f"result{b}_{n}")
                if on_gpsimd:
                    nc.gpsimd.tensor_scalar(result[:], exps[b][:, cols], inverse[:], 0.0, ALU.mult, ALU.add)
                else:
                    nc.vector.tensor_scalar(result[:], exps[b][:, cols], inverse[:], None, ALU.mult)
                nc.sync.dma_start(out[b * P : (b + 1) * P, cols], result[:])

        products("h", [0, 1], ["scalar", "gpsimd"], "stage_first")
        products("g", [0], ["scalar"], "stage_g0")
        products("g", [1], ["vector"], "stage_first")
        first_tap(0)
        first_tap(1)
        products("h", [2, 3], ["vector"], "stage_h2")
        products("g", [2, 3], ["scalar", "gpsimd"], "stage_last")

        lagged_tap(0, 1)
        for b in range(LAST):
            lagged_tap(b + 1, 1)
            lagged_tap(b, 2)
            add_z_on_gpsimd(b)
            if b == 0:
                first_tap(2)
                first_tap(3)

        exponentials(0)
        lagged_tap(LAST, 2)
        normalise(0, on_gpsimd=True, pieces=1)
        exponentials(1)
        add_z_on_vector(LAST)
        exponentials(2)
        exponentials(LAST)
        for b in range(1, BLOCKS):
            normalise(b, on_gpsimd=False, pieces=2 if b == LAST else 1)
